import numpy as np
import ml_dtypes


def mxq(x, axis, fmt="e4m3"):
    dtype, down = {"e4m3": (ml_dtypes.float8_e4m3fn, 7), "e5m2": (ml_dtypes.float8_e5m2, 14)}[fmt]
    v = np.moveaxis(np.asarray(x, np.float32).astype(ml_dtypes.bfloat16).astype(np.float64), axis, -1)
    blocks = v.reshape(v.shape[:-1] + (-1, 32))
    amax = np.abs(blocks).max(-1, keepdims=True)
    byte = np.maximum(np.where(amax > 0, np.frexp(amax)[1] - 1 + 127, 0) - down, 1)
    scale = np.exp2(byte - 127.0)
    codes = (blocks / scale).astype(np.float32).astype(dtype).astype(np.float64)
    return np.moveaxis((codes * scale).reshape(v.shape), -1, axis)


WIDE = False


def mx_kscale(k):
    if not WIDE:
        return np.ones(k)
    levels = np.array([10, -10, 5, -5, 0])
    if k % 512:
        return np.exp2(np.random.permutation(np.resize(levels, k // 32))).repeat(32)
    a = np.empty((k // 512, 16))
    for p in range(k // 512):
        a[p, :8] = np.random.permutation(np.resize(levels, 8))
        for g in range(8):
            far = levels[np.abs(levels - a[p, g]) >= 10]
            a[p, g + 8] = far[np.random.randint(len(far))]
    return np.exp2(a.ravel()).repeat(32)


BF16 = ml_dtypes.bfloat16


def bf(x):
    return np.asarray(x, np.float32).astype(BF16)


def f64(x):
    return np.asarray(x).astype(np.float64)


E2M1 = np.array([0.0, 0.5, 1.0, 1.5, 2.0, 3.0, 4.0, 6.0, -0.0, -0.5, -1.0, -1.5, -2.0, -3.0, -4.0, -6.0])


def pack_weight(w, fmt):
    k, n = w.shape
    w = f64(bf(w)).reshape(k // 32, 32, n)
    amax = np.abs(w).max(1)
    if fmt == "e4m3":
        byte = np.frexp(amax)[1] - 1 + 127 - 7
    else:
        mant, ex = np.frexp(amax / 6.0)
        byte = np.where(mant > 0.5, ex, ex - 1) + 127
    byte = np.clip(np.where(amax > 0, byte, 1), 1, 254)
    scaled = (w * np.exp2(127.0 - byte)[:, None, :]).reshape(k, n).astype(np.float32)
    by_word = np.ascontiguousarray(scaled.reshape(k // 512, 128, 4, n).transpose(0, 1, 3, 2))
    if fmt == "e4m3":
        words = by_word.astype(ml_dtypes.float8_e4m3fn).view(np.uint8)
    else:
        c = by_word.astype(ml_dtypes.float4_e2m1fn).view(np.uint8) & 0xF
        words = c[..., 0::2] | (c[..., 1::2] << 4)
    return np.ascontiguousarray(words), np.ascontiguousarray(byte.astype(np.uint8).reshape(k // 512, 16, n))


def unpack_weight(words, scales, fmt):
    g, p, n, _ = words.shape
    if fmt == "e4m3":
        vals = np.ascontiguousarray(words).view(ml_dtypes.float8_e4m3fn).astype(np.float64)
    else:
        nib = np.empty((g, p, n, 4), np.uint8)
        nib[..., 0::2] = words & 0xF
        nib[..., 1::2] = words >> 4
        vals = E2M1[nib]
    vals = vals * np.repeat(np.exp2(scales.astype(np.float64) - 127.0), 8, axis=1)[..., None]
    return vals.transpose(0, 1, 3, 2).reshape(g * 512, n)
def pack4(w):
    words, scales = pack_weight(w, "e2m1")
    return words.reshape(words.shape[0], 128, -1), scales


def unpack4(words, scales):
    return unpack_weight(words.reshape(words.shape[0], 128, -1, 2), scales, "e2m1")


T, C, D, H, F = 2048, 512, 1024, 256, 1024


def draw0():
    s, u, t = mx_kscale(C), mx_kscale(D), mx_kscale(T)
    z = np.random.standard_normal((T, C)) * s * t[:, None]
    attn_w = np.random.standard_normal((C, H)) * 4 / np.sqrt(C * T) / s[:, None]
    x = np.random.standard_normal((T, D)) * u
    proj = np.random.standard_normal((D, F)) / np.sqrt(D) / u[:, None]
    conf = np.random.uniform(0.2, 1.8, T) * 4 / np.sqrt(T) / t
    proj_words, proj_scales = pack4(proj)
    return {"z": bf(z), "attn_w": bf(attn_w), "x": bf(x),
            "proj_words": proj_words, "proj_scales": proj_scales, "conf": bf(conf)}


def core(z, attn_w, x, proj_words, proj_scales, conf):
    score = mxq(f64(z), 1, "e4m3") @ mxq(f64(attn_w), 0, "e4m3")
    a = np.maximum(score, 0.0)
    v = mxq(f64(x), 1, "e4m3") @ unpack4(proj_words, proj_scales)
    f = v * f64(conf)[:, None]
    e = f * v
    qa = mxq(a, 0, "e4m3")
    first = qa.T @ mxq(f, 0, "e4m3")
    second = qa.T @ mxq(e, 0, "e4m3")
    return first, second


def e4m3fn_bytes(y):
    return np.clip(np.asarray(y, np.float64), -448.0, 448.0).astype(np.float32).astype(ml_dtypes.float8_e4m3fn).view(np.uint8)


def e4m3fn_values(b):
    return np.asarray(b, np.uint8).view(ml_dtypes.float8_e4m3fn).astype(np.float64)


def setup_inputs():
    d = draw0()
    x0 = np.asarray(d['x']).astype(np.float64)
    s = (np.max(np.abs(x0), axis=(0,), keepdims=True) / 448.0).astype(np.float32)
    out = {}
    for k, v in d.items():
        if k == 'x':
            out['x_bytes'] = e4m3fn_bytes(x0 / s.astype(np.float64))
            out['x_scale'] = s
        else:
            out[k] = v
    return out


def reference(z, attn_w, x_bytes, x_scale, proj_words, proj_scales, conf):
    return core(z, attn_w, e4m3fn_values(x_bytes) * x_scale.astype(np.float64), proj_words, proj_scales, conf)

@@ -1,0 +1,420 @@
+from contextlib import ExitStack
+
+import concourse.mybir as mybir
+from concourse.masks import make_identity
+
+T, C, D, H, F = 2048, 512, 1024, 256, 1024
+FLOPS = 2 * T * C * H + 2 * T * D * F + 2 * 2 * T * H * F
+
+F32 = mybir.dt.float32
+BF16 = mybir.dt.bfloat16
+U32 = mybir.dt.uint32
+I32 = mybir.dt.int32
+U8 = mybir.dt.uint8
+FP8 = mybir.dt.float8_e4m3fn
+FP8X4 = mybir.dt.float8_e4m3fn_x4
+FP4X4 = mybir.dt.float4_e2m1fn_x4
+ALU = mybir.AluOpType
+ACT = mybir.ActivationFunctionType
+
+P = 128
+G = 4
+TT = 4
+CH = 128
+NQ = 32
+
+EI_ON_VECTOR = (False, False, False, False, True, False, True)
+
+
+def tile_phonetic_attention_statistics_poolin_s11_kernel(
+    tc, z, attn_w, x_bytes, x_scale, proj_words, proj_scales, conf, out_0, out_1
+):
+    nc = tc.nc
+    outs = (out_0, out_1)
+    with ExitStack() as ctx:
+        keep = ctx.enter_context(tc.tile_pool(name="keep", bufs=1))
+        stage = ctx.enter_context(tc.tile_pool(name="stage", bufs=3))
+        psum = ctx.enter_context(tc.psum_pool(name="psum", bufs=1))
+
+        def kept(tag, shape, dtype):
+            return keep.tile(shape, dtype, name=tag, tag=tag, align_bytes=64)
+
+        def staged(tag, shape, dtype, bufs=3):
+            return stage.tile(shape, dtype, name=tag, tag=tag, bufs=bufs, align_bytes=64)
+
+        def bank(k):
+            tag = "bank" + str(k)
+            return psum.tile([P, 512], F32, name=tag, tag=tag)
+
+        ident = kept("ident", [P, P], F32)
+        w_sc = kept("w_sc", [P, 2, F], U8)
+        warm = kept("warm", [P, 1], F32)
+        half = kept("half", [P, G * TT], F32)
+        nc.gpsimd.memset(warm[:], 0.0)
+        nc.gpsimd.memset(w_sc[:].rearrange("p g n -> p (g n)").bitcast(I32), 0)
+        nc.gpsimd.memset(half[:], 0.5)
+        make_identity(nc, ident[:])
+        warm2 = kept("warm2", [P, 1], F32)
+        nc.scalar.activation(warm2[:], warm[:], ACT.Square)
+
+        xs = kept("xs", [P, D], F32)
+        nc.scalar.dma_start(out=xs[:], in_=x_scale.rearrange("o k -> (o k)").partition_broadcast(P))
+        conf_b = kept("conf_b", [P, G, TT], BF16)
+        aw_raw = kept("aw_raw", [P, 4, H], BF16)
+        zv = z.rearrange("(g m t) k -> g m t k", m=P, t=TT)
+        xv = x_bytes.rearrange("(g m t) k -> g m t k", m=P, t=TT)
+        z_raw, x_raw = {}, {}
+
+        def load_z(i):
+            z_raw[i] = kept("z_raw" + str(i), [P, 2, C], BF16)
+            nc.sync.dma_start(out=z_raw[i][:], in_=zv[i // 2, :, 2 * (i % 2) : 2 * (i % 2) + 2, :])
+
+        def load_x(i):
+            x_raw[i] = kept("x_raw" + str(i), [P, 2, D], U8)
+            nc.sync.dma_start(out=x_raw[i][:], in_=xv[i // 2, :, 2 * (i % 2) : 2 * (i % 2) + 2, :])
+
+        load_x(0)
+        nc.sync.dma_start(out=aw_raw[:], in_=attn_w.rearrange("(p j) h -> p j h", j=4))
+        load_z(0)
+        load_z(1)
+        load_x(1)
+        load_z(2)
+        load_x(2)
+        load_z(3)
+        load_x(3)
+        nc.gpsimd.dma_start(out=conf_b[:], in_=conf.rearrange("(g p t) -> p g t", p=P, t=TT))
+        for q in range(4):
+            nc.sync.dma_start(
+                out=w_sc[32 * q : 32 * q + 4, :, :].bitcast(I32),
+                in_=proj_scales[:, 4 * q : 4 * q + 4, :].bitcast(I32).rearrange("g q n -> q g n"),
+            )
+        w_words = kept("w_words", [P, 2, 2 * F], U8)
+        nc.sync.dma_start(out=w_words[:], in_=proj_words.rearrange("g p n -> p g n"))
+        for i in range(4, 8):
+            load_z(i)
+            load_x(i)
+
+        conf_f = kept("conf_f", [P, G, TT], F32)
+        root = kept("root", [P, G, TT], F32)
+
+        aw_codes = kept("aw_codes", [P, H], U32)
+        aw_sc = kept("aw_sc", [P, H], U8)
+        z_codes = [kept("z_codes" + str(g), [P, TT, P], U32) for g in range(G)]
+        z_sc = [kept("z_sc" + str(g), [P, TT, P], U8) for g in range(G)]
+        x_codes = [kept("x_codes" + str(i), [P, 2, 2, P], U32) for i in range(2 * G)]
+        x_sc = [kept("x_sc" + str(i), [P, 2, 2, P], U8) for i in range(2 * G)]
+        a_codes = [kept("a_codes" + str(g), [P, H], U32) for g in range(G)]
+        a_sc = [kept("a_sc" + str(g), [P, H], U8) for g in range(G)]
+        f_codes = [kept("f_codes" + str(u), [P, 512], U32) for u in range(8)]
+        f_sc = [kept("f_sc" + str(u), [P, 512], U8) for u in range(8)]
+        e_codes = [kept("e_codes" + str(u), [P, 512], U32) for u in range(8)]
+        e_sc = [kept("e_sc" + str(u), [P, 512], U8) for u in range(8)]
+
+        def quantize(codes, scales, rows):
+            nc.vector.quantize_mx(out=codes.bitcast(FP8X4), scales=scales, in_=rows)
+
+        xb, xt_bank, x_grp = {}, {}, {}
+
+        def widen_x(i):
+            xb[i] = staged("xb", [P, D], BF16, 4)
+            nc.vector.tensor_tensor(
+                out=xb[i][:], in0=x_raw[i // 2][:, i % 2, :].bitcast(FP8), in1=xs[:], op=ALU.mult
+            )
+
+        def transpose_x(i):
+            xt_bank[i] = bank(i % 2)
+            words = xb[i][:].bitcast(F32)
+            for q in range(2):
+                for u in range(2):
+                    s = 2 * q + u
+                    nc.tensor.transpose(
+                        xt_bank[i][:, P * s : P * (s + 1)], words[:, 256 * q + u : 256 * (q + 1) : 2], ident[:]
+                    )
+
+        def collect_x(i):
+            if i % 2 == 0:
+                x_grp[i // 2] = staged("x_grp", [P, 2, 2, P, 4], BF16)
+            dst = x_grp[i // 2][:, i % 2].rearrange("p q r t -> p (q r t)").bitcast(F32)
+            nc.scalar.copy(
+                out=dst.rearrange("p (q r u) -> p q r u", q=2, u=2),
+                in_=xt_bank[i][:].rearrange("p (q u r) -> p q r u", q=2, u=2),
+            )
+
+        def quantize_x(k):
+            quantize(
+                x_codes[k][:].rearrange("p i q r -> p (i q r)"),
+                x_sc[k][:].rearrange("p i q r -> p (i q r)"),
+                x_grp[k][:].rearrange("p i q r t -> p (i q r t)"),
+            )
+
+        z_bank, z_grp, a_bank, a_grp = {}, {}, {}, {}
+
+        def transpose_z(i):
+            z_bank[i] = bank(2 + i % 2)
+            for t in range(2):
+                words = z_raw[i][:, t, :].bitcast(F32)
+                for u in range(2):
+                    s = 2 * t + u
+                    nc.tensor.transpose(z_bank[i][:, P * s : P * (s + 1)], words[:, u:256:2], ident[:])
+
+        def collect_z(i):
+            g = i // 2
+            if i % 2 == 0:
+                z_grp[g] = staged("z_grp", [P, TT, P, 4], BF16, 2)
+            dst = z_grp[g][:, 2 * (i % 2) : 2 * (i % 2) + 2].rearrange("p q r t -> p (q r t)").bitcast(F32)
+            nc.scalar.copy(
+                out=dst.rearrange("p (q r u) -> p q r u", q=2, u=2),
+                in_=z_bank[i][:].rearrange("p (q u r) -> p q r u", q=2, u=2),
+            )
+
+        def quantize_z(g):
+            quantize(
+                z_codes[g][:].rearrange("p t r -> p (t r)"),
+                z_sc[g][:].rearrange("p t r -> p (t r)"),
+                z_grp[g][:].rearrange("p t r j -> p (t r j)"),
+            )
+
+        def score(i):
+            g, h = i // 2, i % 2
+            a_bank[i] = bank(2 + i % 2)
+            cols = slice(P * h, P * (h + 1))
+            for t in range(TT):
+                nc.tensor.matmul_mx(
+                    out=a_bank[i][:, P * t : P * (t + 1)],
+                    lhsT=z_codes[g][:, t, :].bitcast(FP8X4),
+                    lhsT_scale=z_sc[g][:, t, :],
+                    rhs=aw_codes[:, cols].bitcast(FP8X4),
+                    rhs_scale=aw_sc[:, cols],
+                    start=True,
+                    stop=True,
+                )
+
+        def relu(i):
+            g, h = i // 2, i % 2
+            if h == 0:
+                a_grp[g] = staged("a_grp", [P, H, TT], BF16, 2)
+            nc.scalar.activation(
+                a_grp[g][:, P * h : P * (h + 1), :], a_bank[i][:].rearrange("p (t n) -> p n t", t=TT), ACT.Relu
+            )
+
+        def quantize_a(g):
+            quantize(a_codes[g][:], a_sc[g][:], a_grp[g][:].rearrange("p h t -> p (h t)"))
+
+        def quad(v):
+            unit, j = v // 4, v % 4
+            return (unit, j, unit, j) if unit < 4 else (unit, j, j, unit)
+
+        v_bank, f_grp, e_pln, e_grp = {}, {}, {}, {}
+
+        def product(v):
+            unit, j, g, c = quad(v)
+            v_bank[v] = bank(4 + v % 4)
+            for t in range(TT):
+                for q in range(2):
+                    k = 2 * g + t // 2
+                    nc.tensor.matmul_mx(
+                        out=v_bank[v][:, P * t : P * (t + 1)],
+                        lhsT=x_codes[k][:, t % 2, q, :].bitcast(FP8X4),
+                        lhsT_scale=x_sc[k][:, t % 2, q, :],
+                        rhs=w_words[:, q, 2 * CH * c : 2 * CH * (c + 1)].bitcast(FP4X4),
+                        rhs_scale=w_sc[:, q, CH * c : CH * (c + 1)],
+                        start=q == 0,
+                        stop=q == 1,
+                    )
+
+        def frames(v):
+            unit, j, g, c = quad(v)
+            if j == 0:
+                f_grp[unit] = staged("f_grp", [P, 512, TT], BF16)
+            nc.vector.tensor_tensor(
+                out=f_grp[unit][:, CH * j : CH * (j + 1), :],
+                in0=v_bank[v][:].rearrange("p (t n) -> p n t", t=TT),
+                in1=conf_f[:, g, :].unsqueeze(1).to_broadcast([P, CH, TT]),
+                op=ALU.mult,
+            )
+
+        def squares(v):
+            unit, j, g, c = quad(v)
+            if j == 0:
+                e_pln[unit] = staged("e_pln", [P, TT, 512], BF16)
+            for t in range(TT):
+                nc.scalar.activation(
+                    e_pln[unit][:, t, CH * j : CH * (j + 1)],
+                    v_bank[v][:, P * t : P * (t + 1)],
+                    ACT.Square,
+                    scale=root[:, g, t : t + 1],
+                )
+
+        def interleave(unit, cols, on_vector):
+            if unit not in e_grp:
+                e_grp[unit] = staged("e_grp", [P, 512, TT], BF16)
+            dst = e_grp[unit][:, cols, :].rearrange("p (c i) t -> p c t i", i=4)
+            src = e_pln[unit][:, :, cols].rearrange("p t (c i) -> p c t i", i=4)
+            if on_vector:
+                nc.vector.tensor_copy(out=dst, in_=src)
+            else:
+                nc.scalar.copy(out=dst, in_=src)
+
+        def quantize_f(unit, cols):
+            quantize(f_codes[unit][:, cols], f_sc[unit][:, cols], f_grp[unit][:, cols, :].rearrange("p n t -> p (n t)"))
+
+        def quantize_e(unit, cols):
+            quantize(e_codes[unit][:, cols], e_sc[unit][:, cols], e_grp[unit][:, cols, :].rearrange("p n t -> p (n t)"))
+
+        def pool_pass(out, s, m, g, unit, cols, start, stop):
+            codes, scales = ((f_codes, f_sc), (e_codes, e_sc))[s]
+            nc.tensor.matmul_mx(
+                out=out,
+                lhsT=a_codes[g][:, P * m : P * (m + 1)].bitcast(FP8X4),
+                lhsT_scale=a_sc[g][:, P * m : P * (m + 1)],
+                rhs=codes[unit][:, cols].bitcast(FP8X4),
+                rhs_scale=scales[unit][:, cols],
+                start=start,
+                stop=stop,
+            )
+
+        acc = {}
+
+        def pool_half(g):
+            for s in range(2):
+                for m in range(2):
+                    if g == 0:
+                        acc[s, m] = bank(2 * s + m)
+                    pool_pass(acc[s, m][:], s, m, g, g, slice(0, 512), g == 0, g == G - 1)
+
+        def emit_half(s, m):
+            res = staged("res_half", [P, 512], F32, 4)
+            if s == 0:
+                nc.scalar.copy(out=res[:], in_=acc[s, m][:])
+            else:
+                nc.vector.tensor_copy(out=res[:], in_=acc[s, m][:])
+            nc.sync.dma_start(out=outs[s][P * m : P * (m + 1), 0:512], in_=res[:])
+
+        def pool_chunk(unit):
+            acc[unit] = bank(unit - 4)
+            for s in range(2):
+                for m in range(2):
+                    o = 2 * s + m
+                    for g in range(G):
+                        pool_pass(
+                            acc[unit][:, P * o : P * (o + 1)], s, m, g, unit, slice(CH * g, CH * (g + 1)), g == 0, g == G - 1
+                        )
+
+        def emit_chunk(unit, on_vector):
+            res = staged("res_chunk", [P, 4, CH], F32, 2)
+            src = acc[unit][:].rearrange("p (o n) -> p o n", o=4)
+            if on_vector:
+                nc.vector.tensor_copy(out=res[:], in_=src)
+            else:
+                nc.scalar.copy(out=res[:], in_=src)
+            for s in range(2):
+                nc.sync.dma_start(
+                    out=outs[s].rearrange("(m p) n -> p m n", p=P)[:, :, CH * unit : CH * (unit + 1)],
+                    in_=res[:, 2 * s : 2 * s + 2, :],
+                )
+
+        last = {}
+
+        def pool_last(gs):
+            for s in range(2):
+                for m in range(2):
+                    if gs[0] == 0:
+                        last[s, m] = bank((3, 0, 1, 4)[2 * s + m])
+                    for g in gs:
+                        pool_pass(
+                            last[s, m][:, 0:CH], s, m, g, 7, slice(CH * g, CH * (g + 1)), g == 0, g == G - 1
+                        )
+
+        def emit_last():
+            for s in range(2):
+                res = staged("res_last", [P, 2, CH], F32, 2)
+                for m in range(2):
+                    if s == 0:
+                        nc.scalar.copy(out=res[:, m, :], in_=last[s, m][:, 0:CH])
+                    else:
+                        nc.vector.tensor_copy(out=res[:, m, :], in_=last[s, m][:, 0:CH])
+                nc.sync.dma_start(
+                    out=outs[s].rearrange("(m p) n -> p m n", p=P)[:, :, CH * 7 : CH * 8], in_=res[:]
+                )
+
+        z_steps = {0: [0], 1: [1], 2: [2], 3: [3, 4], 4: [5], 5: [6], 6: [7]}
+        zq_steps = {2: 0, 4: 1, 6: 2, 8: 3}
+        score_steps = {4: 0, 5: 1, 6: 2, 7: 3, 8: 4, 9: 5, 10: 6, 11: 7}
+        aq_steps = {7: 0, 9: 1, 11: 2, 13: 3}
+        whole = slice(0, 512)
+
+        with ExitStack():
+            aw_grp = kept("aw_grp", [P, H, 4], BF16)
+            nc.vector.tensor_copy(out=aw_grp[:], in_=aw_raw[:].rearrange("p j h -> p h j"))
+            nc.vector.tensor_copy(out=conf_f[:], in_=conf_b[:])
+            nc.gpsimd.tensor_tensor(
+                out=root[:].rearrange("p g t -> p (g t)"),
+                in0=conf_f[:].rearrange("p g t -> p (g t)"),
+                in1=half[:],
+                op=ALU.pow,
+            )
+            quantize(aw_codes[:], aw_sc[:], aw_grp[:].rearrange("p h j -> p (h j)"))
+            for i in range(42):
+                for k in z_steps.get(i, []):
+                    transpose_z(k)
+                    collect_z(k)
+                if 0 <= i - 6 < NQ:
+                    product(i - 6)
+                if 1 <= i <= 16:
+                    transpose_x(i - 1)
+                    collect_x(i - 1)
+                if i in score_steps:
+                    score(score_steps[i])
+                if 0 <= i - 7 < NQ:
+                    frames(i - 7)
+                if i < 16:
+                    widen_x(i)
+                if 0 <= i - 8 < NQ:
+                    squares(i - 8)
+                if i in score_steps:
+                    relu(score_steps[i])
+                if i % 2 == 1 and 3 <= i <= 17:
+                    quantize_x((i - 3) // 2)
+                if i in zq_steps:
+                    quantize_z(zq_steps[i])
+                if i in aq_steps:
+                    quantize_a(aq_steps[i])
+                for unit in range(7):
+                    if i == 4 * unit + 11:
+                        quantize_f(unit, whole)
+                    if i == 4 * unit + 12:
+                        interleave(unit, whole, EI_ON_VECTOR[unit])
+                    if i == 4 * unit + 13:
+                        quantize_e(unit, whole)
+                if i == 37:
+                    quantize_f(7, slice(0, 256))
+                if i == 38:
+                    interleave(7, slice(0, 256), True)
+                if i == 39:
+                    quantize_f(7, slice(256, 512))
+                    quantize_e(7, slice(0, 256))
+                if i == 40:
+                    pool_last((0, 1))
+                    interleave(7, slice(256, 384), True)
+                    interleave(7, slice(384, 512), False)
+                    quantize_e(7, slice(256, 512))
+                    pool_last((2, 3))
+                    emit_last()
+                if i == 18:
+                    pool_half(0)
+                if i == 19:
+                    pool_half(1)
+                if i == 22:
+                    pool_half(2)
+                if i == 26:
+                    pool_half(3)
+                if i == 27:
+                    emit_half(0, 0)
+                    emit_half(1, 0)
+                if i == 28:
+                    emit_half(0, 1)
+                    emit_half(1, 1)
+                if i in (30, 34, 38):
+                    pool_chunk((i - 14) // 4)
+                if i in (31, 35, 39):
+                    emit_chunk((i - 15) // 4, i == 35)

@@ -23,7 +23,7 @@ TT = 4
 CH = 128
 NQ = 32
 
-EI_ON_VECTOR = (False, False, False, False, True, False, True)
+EI_ENGINE = ("s", "s", "s", "s", "g", "g", "g")
 
 
 def tile_phonetic_attention_statistics_poolin_s11_kernel(
@@ -61,6 +61,7 @@ def tile_phonetic_attention_statistics_poolin_s11_kernel(
         nc.scalar.dma_start(out=xs[:], in_=x_scale.rearrange("o k -> (o k)").partition_broadcast(P))
         conf_b = kept("conf_b", [P, G, TT], BF16)
         aw_raw = kept("aw_raw", [P, 4, H], BF16)
+        nc.sync.dma_start(out=aw_raw[:], in_=attn_w.rearrange("(p j) h -> p j h", j=4))
         zv = z.rearrange("(g m t) k -> g m t k", m=P, t=TT)
         xv = x_bytes.rearrange("(g m t) k -> g m t k", m=P, t=TT)
         z_raw, x_raw = {}, {}
@@ -73,9 +74,8 @@ def tile_phonetic_attention_statistics_poolin_s11_kernel(
             x_raw[i] = kept("x_raw" + str(i), [P, 2, D], U8)
             nc.sync.dma_start(out=x_raw[i][:], in_=xv[i // 2, :, 2 * (i % 2) : 2 * (i % 2) + 2, :])
 
-        load_x(0)
-        nc.sync.dma_start(out=aw_raw[:], in_=attn_w.rearrange("(p j) h -> p j h", j=4))
         load_z(0)
+        load_x(0)
         load_z(1)
         load_x(1)
         load_z(2)
@@ -245,15 +245,24 @@ def tile_phonetic_attention_statistics_poolin_s11_kernel(
                     scale=root[:, g, t : t + 1],
                 )
 
-        def interleave(unit, cols, on_vector):
+        def interleave(unit, cols, engine):
             if unit not in e_grp:
                 e_grp[unit] = staged("e_grp", [P, 512, TT], BF16)
             dst = e_grp[unit][:, cols, :].rearrange("p (c i) t -> p c t i", i=4)
             src = e_pln[unit][:, :, cols].rearrange("p t (c i) -> p c t i", i=4)
-            if on_vector:
+            if engine == "v":
                 nc.vector.tensor_copy(out=dst, in_=src)
-            else:
+            elif engine == "s":
                 nc.scalar.copy(out=dst, in_=src)
+            else:
+                nc.gpsimd.tensor_scalar(
+                    out=e_grp[unit][:, cols, :],
+                    in0=e_pln[unit][:, :, cols].rearrange("p t n -> p n t"),
+                    scalar1=1.0,
+                    scalar2=0.0,
+                    op0=ALU.mult,
+                    op1=ALU.add,
+                )
 
         def quantize_f(unit, cols):
             quantize(f_codes[unit][:, cols], f_sc[unit][:, cols], f_grp[unit][:, cols, :].rearrange("p n t -> p (n t)"))
@@ -382,21 +391,25 @@ def tile_phonetic_attention_statistics_poolin_s11_kernel(
                 for unit in range(7):
                     if i == 4 * unit + 11:
                         quantize_f(unit, whole)
-                    if i == 4 * unit + 12:
-                        interleave(unit, whole, EI_ON_VECTOR[unit])
+                    if i == 4 * unit + 12 and EI_ENGINE[unit] != "g":
+                        interleave(unit, whole, EI_ENGINE[unit])
+                    if 4 * unit + 8 <= i < 4 * unit + 12 and EI_ENGINE[unit] == "g":
+                        j = i - 4 * unit - 8
+                        interleave(unit, slice(CH * j, CH * (j + 1)), "g")
                     if i == 4 * unit + 13:
                         quantize_e(unit, whole)
                 if i == 37:
                     quantize_f(7, slice(0, 256))
                 if i == 38:
-                    interleave(7, slice(0, 256), True)
+                    interleave(7, slice(0, 128), "g")
+                    interleave(7, slice(128, 256), "g")
                 if i == 39:
                     quantize_f(7, slice(256, 512))
                     quantize_e(7, slice(0, 256))
                 if i == 40:
                     pool_last((0, 1))
-                    interleave(7, slice(256, 384), True)
-                    interleave(7, slice(384, 512), False)
+                    interleave(7, slice(256, 384), "v")
+                    interleave(7, slice(384, 512), "v")
                     quantize_e(7, slice(256, 512))
                     pool_last((2, 3))
                     emit_last()
@@ -417,4 +430,4 @@ def tile_phonetic_attention_statistics_poolin_s11_kernel(
                 if i in (30, 34, 38):
                     pool_chunk((i - 14) // 4)
                 if i in (31, 35, 39):
-                    emit_chunk((i - 15) // 4, i == 35)
+                    emit_chunk((i - 15) // 4, False)

@@ -23,7 +23,8 @@ TT = 4
 CH = 128
 NQ = 32
 
-EI_ENGINE = ("s", "s", "s", "s", "g", "g", "g")
+EI_ENGINE = ("g", "g", "g", "g", "g", "g", "g")
+CAST_ENGINE = "vs" + 14 * "s"
 
 
 def tile_phonetic_attention_statistics_poolin_s11_kernel(
@@ -57,11 +58,10 @@ def tile_phonetic_attention_statistics_poolin_s11_kernel(
         warm2 = kept("warm2", [P, 1], F32)
         nc.scalar.activation(warm2[:], warm[:], ACT.Square)
 
-        xs = kept("xs", [P, D], F32)
-        nc.scalar.dma_start(out=xs[:], in_=x_scale.rearrange("o k -> (o k)").partition_broadcast(P))
+        xs = kept("xs", [P, 2, 4], F32)
+        nc.scalar.dma_start(out=xs[:], in_=x_scale[0, :].rearrange("(g p t) -> p g t", p=P, t=4))
         conf_b = kept("conf_b", [P, G, TT], BF16)
         aw_raw = kept("aw_raw", [P, 4, H], BF16)
-        nc.sync.dma_start(out=aw_raw[:], in_=attn_w.rearrange("(p j) h -> p j h", j=4))
         zv = z.rearrange("(g m t) k -> g m t k", m=P, t=TT)
         xv = x_bytes.rearrange("(g m t) k -> g m t k", m=P, t=TT)
         z_raw, x_raw = {}, {}
@@ -74,10 +74,11 @@ def tile_phonetic_attention_statistics_poolin_s11_kernel(
             x_raw[i] = kept("x_raw" + str(i), [P, 2, D], U8)
             nc.sync.dma_start(out=x_raw[i][:], in_=xv[i // 2, :, 2 * (i % 2) : 2 * (i % 2) + 2, :])
 
-        load_z(0)
         load_x(0)
-        load_z(1)
+        nc.sync.dma_start(out=aw_raw[:], in_=attn_w.rearrange("(p j) h -> p j h", j=4))
+        load_z(0)
         load_x(1)
+        load_z(1)
         load_z(2)
         load_x(2)
         load_z(3)
@@ -117,9 +118,11 @@ def tile_phonetic_attention_statistics_poolin_s11_kernel(
 
         def widen_x(i):
             xb[i] = staged("xb", [P, D], BF16, 4)
-            nc.vector.tensor_tensor(
-                out=xb[i][:], in0=x_raw[i // 2][:, i % 2, :].bitcast(FP8), in1=xs[:], op=ALU.mult
-            )
+            src = x_raw[i // 2][:, i % 2, :].bitcast(FP8)
+            if CAST_ENGINE[i] == "v":
+                nc.vector.tensor_copy(out=xb[i][:], in_=src)
+            else:
+                nc.scalar.copy(out=xb[i][:], in_=src)
 
         def transpose_x(i):
             xt_bank[i] = bank(i % 2)
@@ -134,11 +137,15 @@ def tile_phonetic_attention_statistics_poolin_s11_kernel(
         def collect_x(i):
             if i % 2 == 0:
                 x_grp[i // 2] = staged("x_grp", [P, 2, 2, P, 4], BF16)
-            dst = x_grp[i // 2][:, i % 2].rearrange("p q r t -> p (q r t)").bitcast(F32)
-            nc.scalar.copy(
-                out=dst.rearrange("p (q r u) -> p q r u", q=2, u=2),
-                in_=xt_bank[i][:].rearrange("p (q u r) -> p q r u", q=2, u=2),
-            )
+            for q in range(2):
+                nc.vector.tensor_tensor(
+                    out=x_grp[i // 2][:, i % 2, q].rearrange("p r (u e) -> p r u e", u=2),
+                    in0=xt_bank[i][:, 256 * q : 256 * (q + 1)]
+                    .bitcast(BF16)
+                    .rearrange("p (u r e) -> p r u e", u=2, e=2),
+                    in1=xs[:, q, :].rearrange("p (u e) -> p u e", u=2).unsqueeze(1).to_broadcast([P, P, 2, 2]),
+                    op=ALU.mult,
+                )
 
         def quantize_x(k):
             quantize(
@@ -353,6 +360,7 @@ def tile_phonetic_attention_statistics_poolin_s11_kernel(
         whole = slice(0, 512)
 
         with ExitStack():
+            widen_x(0)
             aw_grp = kept("aw_grp", [P, H, 4], BF16)
             nc.vector.tensor_copy(out=aw_grp[:], in_=aw_raw[:].rearrange("p j h -> p h j"))
             nc.vector.tensor_copy(out=conf_f[:], in_=conf_b[:])
@@ -376,7 +384,7 @@ def tile_phonetic_attention_statistics_poolin_s11_kernel(
                     score(score_steps[i])
                 if 0 <= i - 7 < NQ:
                     frames(i - 7)
-                if i < 16:
+                if 1 <= i < 16:
                     widen_x(i)
                 if 0 <= i - 8 < NQ:
                     squares(i - 8)

@@ -25,6 +25,7 @@ NQ = 32
 
 EI_ENGINE = ("g", "g", "g", "g", "g", "g", "g")
 CAST_ENGINE = "vs" + 14 * "s"
+DUMMIES = (3, 3, 3, 1, 1, 1, 1, 1)
 
 
 def tile_phonetic_attention_statistics_poolin_s11_kernel(
@@ -47,6 +48,14 @@ def tile_phonetic_attention_statistics_poolin_s11_kernel(
             tag = "bank" + str(k)
             return psum.tile([P, 512], F32, name=tag, tag=tag)
 
+        early = []
+
+        def early_bank():
+            early.append(len(early) % 4)
+            return bank(early[-1])
+
+        zeros = kept("zeros", [P, 512], BF16)
+        nc.vector.memset(zeros[:], 0.0)
         ident = kept("ident", [P, P], F32)
         w_sc = kept("w_sc", [P, 2, F], U8)
         warm = kept("warm", [P, 1], F32)
@@ -114,6 +123,9 @@ def tile_phonetic_attention_statistics_poolin_s11_kernel(
         def quantize(codes, scales, rows):
             nc.vector.quantize_mx(out=codes.bitcast(FP8X4), scales=scales, in_=rows)
 
+        def keep_warm(out):
+            nc.tensor.matmul(out, lhsT=zeros[:, 0:P], rhs=zeros[:], start=True, stop=True)
+
         xb, xt_bank, x_grp = {}, {}, {}
 
         def widen_x(i):
@@ -124,12 +136,14 @@ def tile_phonetic_attention_statistics_poolin_s11_kernel(
             else:
                 nc.scalar.copy(out=xb[i][:], in_=src)
 
-        def transpose_x(i):
-            xt_bank[i] = bank(i % 2)
+        def transpose_x(i, dummies):
+            xt_bank[i] = early_bank()
+            for n in range(dummies):
+                keep_warm(xt_bank[i][:])
             words = xb[i][:].bitcast(F32)
             for q in range(2):
                 for u in range(2):
-                    s = 2 * q + u
+                    s = 2 * u + q
                     nc.tensor.transpose(
                         xt_bank[i][:, P * s : P * (s + 1)], words[:, 256 * q + u : 256 * (q + 1) : 2], ident[:]
                     )
@@ -137,15 +151,12 @@ def tile_phonetic_attention_statistics_poolin_s11_kernel(
         def collect_x(i):
             if i % 2 == 0:
                 x_grp[i // 2] = staged("x_grp", [P, 2, 2, P, 4], BF16)
-            for q in range(2):
-                nc.vector.tensor_tensor(
-                    out=x_grp[i // 2][:, i % 2, q].rearrange("p r (u e) -> p r u e", u=2),
-                    in0=xt_bank[i][:, 256 * q : 256 * (q + 1)]
-                    .bitcast(BF16)
-                    .rearrange("p (u r e) -> p r u e", u=2, e=2),
-                    in1=xs[:, q, :].rearrange("p (u e) -> p u e", u=2).unsqueeze(1).to_broadcast([P, P, 2, 2]),
-                    op=ALU.mult,
-                )
+            nc.vector.tensor_tensor(
+                out=x_grp[i // 2][:, i % 2].rearrange("p q r (u e) -> p q r u e", u=2),
+                in0=xt_bank[i][:].bitcast(BF16).rearrange("p (u q r e) -> p q r u e", u=2, q=2, e=2),
+                in1=xs[:].rearrange("p q (u e) -> p q u e", u=2).unsqueeze(2).to_broadcast([P, 2, P, 2, 2]),
+                op=ALU.mult,
+            )
 
         def quantize_x(k):
             quantize(
@@ -157,7 +168,7 @@ def tile_phonetic_attention_statistics_poolin_s11_kernel(
         z_bank, z_grp, a_bank, a_grp = {}, {}, {}, {}
 
         def transpose_z(i):
-            z_bank[i] = bank(2 + i % 2)
+            z_bank[i] = early_bank()
             for t in range(2):
                 words = z_raw[i][:, t, :].bitcast(F32)
                 for u in range(2):
@@ -183,7 +194,7 @@ def tile_phonetic_attention_statistics_poolin_s11_kernel(
 
         def score(i):
             g, h = i // 2, i % 2
-            a_bank[i] = bank(2 + i % 2)
+            a_bank[i] = early_bank()
             cols = slice(P * h, P * (h + 1))
             for t in range(TT):
                 nc.tensor.matmul_mx(
@@ -300,7 +311,7 @@ def tile_phonetic_attention_statistics_poolin_s11_kernel(
 
         def emit_half(s, m):
             res = staged("res_half", [P, 512], F32, 4)
-            if s == 0:
+            if (s, m) != (1, 1):
                 nc.scalar.copy(out=res[:], in_=acc[s, m][:])
             else:
                 nc.vector.tensor_copy(out=res[:], in_=acc[s, m][:])
@@ -353,45 +364,63 @@ def tile_phonetic_attention_statistics_poolin_s11_kernel(
                     out=outs[s].rearrange("(m p) n -> p m n", p=P)[:, :, CH * 7 : CH * 8], in_=res[:]
                 )
 
-        z_steps = {0: [0], 1: [1], 2: [2], 3: [3, 4], 4: [5], 5: [6], 6: [7]}
-        zq_steps = {2: 0, 4: 1, 6: 2, 8: 3}
-        score_steps = {4: 0, 5: 1, 6: 2, 7: 3, 8: 4, 9: 5, 10: 6, 11: 7}
-        aq_steps = {7: 0, 9: 1, 11: 2, 13: 3}
+        zq_steps = {3: 0, 5: 1, 9: 2, 13: 3}
+        z_runs = {0: [0, 1], 1: [2], 2: [3], 3: [4], 4: [5], 5: [6], 6: [7]}
+        score_runs = {3: [0, 1], 4: [2, 3], 6: [4, 5], 8: [6, 7]}
+        aq_steps = {8: 0, 10: 1, 14: 2, 18: 3}
         whole = slice(0, 512)
 
-        with ExitStack():
+        with tc.manual_schedule(engines={mybir.EngineType.PE}):
+            head = bank(7)
+            for n in range(6):
+                keep_warm(head[:])
             widen_x(0)
+            widen_x(1)
             aw_grp = kept("aw_grp", [P, H, 4], BF16)
-            nc.vector.tensor_copy(out=aw_grp[:], in_=aw_raw[:].rearrange("p j h -> p h j"))
-            nc.vector.tensor_copy(out=conf_f[:], in_=conf_b[:])
+            nc.gpsimd.tensor_scalar(
+                out=aw_grp[:],
+                in0=aw_raw[:].rearrange("p j h -> p h j"),
+                scalar1=1.0,
+                scalar2=0.0,
+                op0=ALU.mult,
+                op1=ALU.add,
+            )
+            nc.gpsimd.tensor_copy(out=conf_f[:], in_=conf_b[:])
             nc.gpsimd.tensor_tensor(
                 out=root[:].rearrange("p g t -> p (g t)"),
                 in0=conf_f[:].rearrange("p g t -> p (g t)"),
                 in1=half[:],
                 op=ALU.pow,
             )
-            quantize(aw_codes[:], aw_sc[:], aw_grp[:].rearrange("p h j -> p (h j)"))
             for i in range(42):
-                for k in z_steps.get(i, []):
-                    transpose_z(k)
-                    collect_z(k)
-                if 0 <= i - 6 < NQ:
-                    product(i - 6)
-                if 1 <= i <= 16:
-                    transpose_x(i - 1)
-                    collect_x(i - 1)
-                if i in score_steps:
-                    score(score_steps[i])
+                d = i // 2
+                if i % 2 == 0:
+                    for k in (i + 2, i + 3):
+                        if k < 16:
+                            widen_x(k)
+                    for k in (i, i + 1):
+                        if k < 16:
+                            transpose_x(k, DUMMIES[d] if k % 2 == 0 else 0)
+                    for k in z_runs.get(d, []):
+                        transpose_z(k)
+                    for k in z_runs.get(d, []):
+                        collect_z(k)
+                    for v in (i - 6, i - 5):
+                        if 0 <= v < NQ:
+                            product(v)
+                    for k in score_runs.get(d, []):
+                        score(k)
+                        relu(k)
+                if i < 16:
+                    collect_x(i)
                 if 0 <= i - 7 < NQ:
                     frames(i - 7)
-                if 1 <= i < 16:
-                    widen_x(i)
                 if 0 <= i - 8 < NQ:
                     squares(i - 8)
-                if i in score_steps:
-                    relu(score_steps[i])
                 if i % 2 == 1 and 3 <= i <= 17:
                     quantize_x((i - 3) // 2)
+                if i == 2:
+                    quantize(aw_codes[:], aw_sc[:], aw_grp[:].rearrange("p h j -> p (h j)"))
                 if i in zq_steps:
                     quantize_z(zq_steps[i])
                 if i in aq_steps:
@@ -416,7 +445,7 @@ def tile_phonetic_attention_statistics_poolin_s11_kernel(
                     quantize_e(7, slice(0, 256))
                 if i == 40:
                     pool_last((0, 1))
-                    interleave(7, slice(256, 384), "v")
+                    interleave(7, slice(256, 384), "g")
                     interleave(7, slice(384, 512), "v")
                     quantize_e(7, slice(256, 512))
                     pool_last((2, 3))

from contextlib import ExitStack

import concourse.mybir as mybir
from concourse.masks import make_identity

T, C, D, H, F = 2048, 512, 1024, 256, 1024
FLOPS = 2 * T * C * H + 2 * T * D * F + 2 * 2 * T * H * F

F32 = mybir.dt.float32
BF16 = mybir.dt.bfloat16
U32 = mybir.dt.uint32
I32 = mybir.dt.int32
U8 = mybir.dt.uint8
FP8 = mybir.dt.float8_e4m3fn
FP8X4 = mybir.dt.float8_e4m3fn_x4
FP4X4 = mybir.dt.float4_e2m1fn_x4
ALU = mybir.AluOpType
ACT = mybir.ActivationFunctionType

P = 128
G = 4
TT = 4
CH = 128
NQ = 32

EI_ENGINE = ("g", "g", "g", "g", "g", "g", "g")
CAST_ENGINE = "vs" + 14 * "s"
DUMMIES = (3, 3, 3, 1, 1, 1, 1, 1)


def tile_phonetic_attention_statistics_poolin_s11_kernel(
    tc, z, attn_w, x_bytes, x_scale, proj_words, proj_scales, conf, out_0, out_1
):
    nc = tc.nc
    outs = (out_0, out_1)
    with ExitStack() as ctx:
        keep = ctx.enter_context(tc.tile_pool(name="keep", bufs=1))
        stage = ctx.enter_context(tc.tile_pool(name="stage", bufs=3))
        psum = ctx.enter_context(tc.psum_pool(name="psum", bufs=1))

        def kept(tag, shape, dtype):
            return keep.tile(shape, dtype, name=tag, tag=tag, align_bytes=64)

        def staged(tag, shape, dtype, bufs=3):
            return stage.tile(shape, dtype, name=tag, tag=tag, bufs=bufs, align_bytes=64)

        def bank(k):
            tag = "bank" + str(k)
            return psum.tile([P, 512], F32, name=tag, tag=tag)

        early = []

        def early_bank():
            early.append(len(early) % 4)
            return bank(early[-1])

        zeros = kept("zeros", [P, 512], BF16)
        nc.vector.memset(zeros[:], 0.0)
        ident = kept("ident", [P, P], F32)
        w_sc = kept("w_sc", [P, 2, F], U8)
        warm = kept("warm", [P, 1], F32)
        half = kept("half", [P, G * TT], F32)
        nc.gpsimd.memset(warm[:], 0.0)
        nc.gpsimd.memset(w_sc[:].rearrange("p g n -> p (g n)").bitcast(I32), 0)
        nc.gpsimd.memset(half[:], 0.5)
        make_identity(nc, ident[:])
        warm2 = kept("warm2", [P, 1], F32)
        nc.scalar.activation(warm2[:], warm[:], ACT.Square)

        xs = kept("xs", [P, 2, 4], F32)
        nc.scalar.dma_start(out=xs[:], in_=x_scale[0, :].rearrange("(g p t) -> p g t", p=P, t=4))
        conf_b = kept("conf_b", [P, G, TT], BF16)
        aw_raw = kept("aw_raw", [P, 4, H], BF16)
        zv = z.rearrange("(g m t) k -> g m t k", m=P, t=TT)
        xv = x_bytes.rearrange("(g m t) k -> g m t k", m=P, t=TT)
        z_raw, x_raw = {}, {}

        def load_z(i):
            z_raw[i] = kept("z_raw" + str(i), [P, 2, C], BF16)
            nc.sync.dma_start(out=z_raw[i][:], in_=zv[i // 2, :, 2 * (i % 2) : 2 * (i % 2) + 2, :])

        def load_x(i):
            x_raw[i] = kept("x_raw" + str(i), [P, 2, D], U8)
            nc.sync.dma_start(out=x_raw[i][:], in_=xv[i // 2, :, 2 * (i % 2) : 2 * (i % 2) + 2, :])

        load_x(0)
        nc.sync.dma_start(out=aw_raw[:], in_=attn_w.rearrange("(p j) h -> p j h", j=4))
        load_z(0)
        load_x(1)
        load_z(1)
        load_z(2)
        load_x(2)
        load_z(3)
        load_x(3)
        nc.gpsimd.dma_start(out=conf_b[:], in_=conf.rearrange("(g p t) -> p g t", p=P, t=TT))
        for q in range(4):
            nc.sync.dma_start(
                out=w_sc[32 * q : 32 * q + 4, :, :].bitcast(I32),
                in_=proj_scales[:, 4 * q : 4 * q + 4, :].bitcast(I32).rearrange("g q n -> q g n"),
            )
        w_words = kept("w_words", [P, 2, 2 * F], U8)
        nc.sync.dma_start(out=w_words[:], in_=proj_words.rearrange("g p n -> p g n"))
        for i in range(4, 8):
            load_z(i)
            load_x(i)

        conf_f = kept("conf_f", [P, G, TT], F32)
        root = kept("root", [P, G, TT], F32)

        aw_codes = kept("aw_codes", [P, H], U32)
        aw_sc = kept("aw_sc", [P, H], U8)
        z_codes = [kept("z_codes" + str(g), [P, TT, P], U32) for g in range(G)]
        z_sc = [kept("z_sc" + str(g), [P, TT, P], U8) for g in range(G)]
        x_codes = [kept("x_codes" + str(i), [P, 2, 2, P], U32) for i in range(2 * G)]
        x_sc = [kept("x_sc" + str(i), [P, 2, 2, P], U8) for i in range(2 * G)]
        a_codes = [kept("a_codes" + str(g), [P, H], U32) for g in range(G)]
        a_sc = [kept("a_sc" + str(g), [P, H], U8) for g in range(G)]
        f_codes = [kept("f_codes" + str(u), [P, 512], U32) for u in range(8)]
        f_sc = [kept("f_sc" + str(u), [P, 512], U8) for u in range(8)]
        e_codes = [kept("e_codes" + str(u), [P, 512], U32) for u in range(8)]
        e_sc = [kept("e_sc" + str(u), [P, 512], U8) for u in range(8)]

        def quantize(codes, scales, rows):
            nc.vector.quantize_mx(out=codes.bitcast(FP8X4), scales=scales, in_=rows)

        def keep_warm(out):
            nc.tensor.matmul(out, lhsT=zeros[:, 0:P], rhs=zeros[:], start=True, stop=True)

        xb, xt_bank, x_grp = {}, {}, {}

        def widen_x(i):
            xb[i] = staged("xb", [P, D], BF16, 4)
            src = x_raw[i // 2][:, i % 2, :].bitcast(FP8)
            if CAST_ENGINE[i] == "v":
                nc.vector.tensor_copy(out=xb[i][:], in_=src)
            else:
                nc.scalar.copy(out=xb[i][:], in_=src)

        def transpose_x(i, dummies):
            xt_bank[i] = early_bank()
            for n in range(dummies):
                keep_warm(xt_bank[i][:])
            words = xb[i][:].bitcast(F32)
            for q in range(2):
                for u in range(2):
                    s = 2 * u + q
                    nc.tensor.transpose(
                        xt_bank[i][:, P * s : P * (s + 1)], words[:, 256 * q + u : 256 * (q + 1) : 2], ident[:]
                    )

        def collect_x(i):
            if i % 2 == 0:
                x_grp[i // 2] = staged("x_grp", [P, 2, 2, P, 4], BF16)
            nc.vector.tensor_tensor(
                out=x_grp[i // 2][:, i % 2].rearrange("p q r (u e) -> p q r u e", u=2),
                in0=xt_bank[i][:].bitcast(BF16).rearrange("p (u q r e) -> p q r u e", u=2, q=2, e=2),
                in1=xs[:].rearrange("p q (u e) -> p q u e", u=2).unsqueeze(2).to_broadcast([P, 2, P, 2, 2]),
                op=ALU.mult,
            )

        def quantize_x(k):
            quantize(
                x_codes[k][:].rearrange("p i q r -> p (i q r)"),
                x_sc[k][:].rearrange("p i q r -> p (i q r)"),
                x_grp[k][:].rearrange("p i q r t -> p (i q r t)"),
            )

        z_bank, z_grp, a_bank, a_grp = {}, {}, {}, {}

        def transpose_z(i):
            z_bank[i] = early_bank()
            for t in range(2):
                words = z_raw[i][:, t, :].bitcast(F32)
                for u in range(2):
                    s = 2 * t + u
                    nc.tensor.transpose(z_bank[i][:, P * s : P * (s + 1)], words[:, u:256:2], ident[:])

        def collect_z(i):
            g = i // 2
            if i % 2 == 0:
                z_grp[g] = staged("z_grp", [P, TT, P, 4], BF16, 2)
            dst = z_grp[g][:, 2 * (i % 2) : 2 * (i % 2) + 2].rearrange("p q r t -> p (q r t)").bitcast(F32)
            nc.scalar.copy(
                out=dst.rearrange("p (q r u) -> p q r u", q=2, u=2),
                in_=z_bank[i][:].rearrange("p (q u r) -> p q r u", q=2, u=2),
            )

        def quantize_z(g):
            quantize(
                z_codes[g][:].rearrange("p t r -> p (t r)"),
                z_sc[g][:].rearrange("p t r -> p (t r)"),
                z_grp[g][:].rearrange("p t r j -> p (t r j)"),
            )

        def score(i):
            g, h = i // 2, i % 2
            a_bank[i] = early_bank()
            cols = slice(P * h, P * (h + 1))
            for t in range(TT):
                nc.tensor.matmul_mx(
                    out=a_bank[i][:, P * t : P * (t + 1)],
                    lhsT=z_codes[g][:, t, :].bitcast(FP8X4),
                    lhsT_scale=z_sc[g][:, t, :],
                    rhs=aw_codes[:, cols].bitcast(FP8X4),
                    rhs_scale=aw_sc[:, cols],
                    start=True,
                    stop=True,
                )

        def relu(i):
            g, h = i // 2, i % 2
            if h == 0:
                a_grp[g] = staged("a_grp", [P, H, TT], BF16, 2)
            nc.scalar.activation(
                a_grp[g][:, P * h : P * (h + 1), :], a_bank[i][:].rearrange("p (t n) -> p n t", t=TT), ACT.Relu
            )

        def quantize_a(g):
            quantize(a_codes[g][:], a_sc[g][:], a_grp[g][:].rearrange("p h t -> p (h t)"))

        def quad(v):
            unit, j = v // 4, v % 4
            return (unit, j, unit, j) if unit < 4 else (unit, j, j, unit)

        v_bank, f_grp, e_pln, e_grp = {}, {}, {}, {}

        def product(v):
            unit, j, g, c = quad(v)
            v_bank[v] = bank(4 + v % 4)
            for t in range(TT):
                for q in range(2):
                    k = 2 * g + t // 2
                    nc.tensor.matmul_mx(
                        out=v_bank[v][:, P * t : P * (t + 1)],
                        lhsT=x_codes[k][:, t % 2, q, :].bitcast(FP8X4),
                        lhsT_scale=x_sc[k][:, t % 2, q, :],
                        rhs=w_words[:, q, 2 * CH * c : 2 * CH * (c + 1)].bitcast(FP4X4),
                        rhs_scale=w_sc[:, q, CH * c : CH * (c + 1)],
                        start=q == 0,
                        stop=q == 1,
                    )

        def frames(v):
            unit, j, g, c = quad(v)
            if j == 0:
                f_grp[unit] = staged("f_grp", [P, 512, TT], BF16)
            nc.vector.tensor_tensor(
                out=f_grp[unit][:, CH * j : CH * (j + 1), :],
                in0=v_bank[v][:].rearrange("p (t n) -> p n t", t=TT),
                in1=conf_f[:, g, :].unsqueeze(1).to_broadcast([P, CH, TT]),
                op=ALU.mult,
            )

        def squares(v):
            unit, j, g, c = quad(v)
            if j == 0:
                e_pln[unit] = staged("e_pln", [P, TT, 512], BF16)
            for t in range(TT):
                nc.scalar.activation(
                    e_pln[unit][:, t, CH * j : CH * (j + 1)],
                    v_bank[v][:, P * t : P * (t + 1)],
                    ACT.Square,
                    scale=root[:, g, t : t + 1],
                )

        def interleave(unit, cols, engine):
            if unit not in e_grp:
                e_grp[unit] = staged("e_grp", [P, 512, TT], BF16)
            dst = e_grp[unit][:, cols, :].rearrange("p (c i) t -> p c t i", i=4)
            src = e_pln[unit][:, :, cols].rearrange("p t (c i) -> p c t i", i=4)
            if engine == "v":
                nc.vector.tensor_copy(out=dst, in_=src)
            elif engine == "s":
                nc.scalar.copy(out=dst, in_=src)
            else:
                nc.gpsimd.tensor_scalar(
                    out=e_grp[unit][:, cols, :],
                    in0=e_pln[unit][:, :, cols].rearrange("p t n -> p n t"),
                    scalar1=1.0,
                    scalar2=0.0,
                    op0=ALU.mult,
                    op1=ALU.add,
                )

        def quantize_f(unit, cols):
            quantize(f_codes[unit][:, cols], f_sc[unit][:, cols], f_grp[unit][:, cols, :].rearrange("p n t -> p (n t)"))

        def quantize_e(unit, cols):
            quantize(e_codes[unit][:, cols], e_sc[unit][:, cols], e_grp[unit][:, cols, :].rearrange("p n t -> p (n t)"))

        def pool_pass(out, s, m, g, unit, cols, start, stop):
            codes, scales = ((f_codes, f_sc), (e_codes, e_sc))[s]
            nc.tensor.matmul_mx(
                out=out,
                lhsT=a_codes[g][:, P * m : P * (m + 1)].bitcast(FP8X4),
                lhsT_scale=a_sc[g][:, P * m : P * (m + 1)],
                rhs=codes[unit][:, cols].bitcast(FP8X4),
                rhs_scale=scales[unit][:, cols],
                start=start,
                stop=stop,
            )

        acc = {}

        def pool_half(g):
            for s in range(2):
                for m in range(2):
                    if g == 0:
                        acc[s, m] = bank(2 * s + m)
                    pool_pass(acc[s, m][:], s, m, g, g, slice(0, 512), g == 0, g == G - 1)

        def emit_half(s, m):
            res = staged("res_half", [P, 512], F32, 4)
            if (s, m) != (1, 1):
                nc.scalar.copy(out=res[:], in_=acc[s, m][:])
            else:
                nc.vector.tensor_copy(out=res[:], in_=acc[s, m][:])
            nc.sync.dma_start(out=outs[s][P * m : P * (m + 1), 0:512], in_=res[:])

        def pool_chunk(unit):
            acc[unit] = bank(unit - 4)
            for s in range(2):
                for m in range(2):
                    o = 2 * s + m
                    for g in range(G):
                        pool_pass(
                            acc[unit][:, P * o : P * (o + 1)], s, m, g, unit, slice(CH * g, CH * (g + 1)), g == 0, g == G - 1
                        )

        def emit_chunk(unit, on_vector):
            res = staged("res_chunk", [P, 4, CH], F32, 2)
            src = acc[unit][:].rearrange("p (o n) -> p o n", o=4)
            if on_vector:
                nc.vector.tensor_copy(out=res[:], in_=src)
            else:
                nc.scalar.copy(out=res[:], in_=src)
            for s in range(2):
                nc.sync.dma_start(
                    out=outs[s].rearrange("(m p) n -> p m n", p=P)[:, :, CH * unit : CH * (unit + 1)],
                    in_=res[:, 2 * s : 2 * s + 2, :],
                )

        last = {}

        def pool_last(gs):
            for s in range(2):
                for m in range(2):
                    if gs[0] == 0:
                        last[s, m] = bank((3, 0, 1, 4)[2 * s + m])
                    for g in gs:
                        pool_pass(
                            last[s, m][:, 0:CH], s, m, g, 7, slice(CH * g, CH * (g + 1)), g == 0, g == G - 1
                        )

        def emit_last():
            for s in range(2):
                res = staged("res_last", [P, 2, CH], F32, 2)
                for m in range(2):
                    if s == 0:
                        nc.scalar.copy(out=res[:, m, :], in_=last[s, m][:, 0:CH])
                    else:
                        nc.vector.tensor_copy(out=res[:, m, :], in_=last[s, m][:, 0:CH])
                nc.sync.dma_start(
                    out=outs[s].rearrange("(m p) n -> p m n", p=P)[:, :, CH * 7 : CH * 8], in_=res[:]
                )

        zq_steps = {3: 0, 5: 1, 9: 2, 13: 3}
        z_runs = {0: [0, 1], 1: [2], 2: [3], 3: [4], 4: [5], 5: [6], 6: [7]}
        score_runs = {3: [0, 1], 4: [2, 3], 6: [4, 5], 8: [6, 7]}
        aq_steps = {8: 0, 10: 1, 14: 2, 18: 3}
        whole = slice(0, 512)

        with tc.manual_schedule(engines={mybir.EngineType.PE}):
            head = bank(7)
            for n in range(6):
                keep_warm(head[:])
            widen_x(0)
            widen_x(1)
            aw_grp = kept("aw_grp", [P, H, 4], BF16)
            nc.gpsimd.tensor_scalar(
                out=aw_grp[:],
                in0=aw_raw[:].rearrange("p j h -> p h j"),
                scalar1=1.0,
                scalar2=0.0,
                op0=ALU.mult,
                op1=ALU.add,
            )
            nc.gpsimd.tensor_copy(out=conf_f[:], in_=conf_b[:])
            nc.gpsimd.tensor_tensor(
                out=root[:].rearrange("p g t -> p (g t)"),
                in0=conf_f[:].rearrange("p g t -> p (g t)"),
                in1=half[:],
                op=ALU.pow,
            )
            for i in range(42):
                d = i // 2
                if i % 2 == 0:
                    for k in (i + 2, i + 3):
                        if k < 16:
                            widen_x(k)
                    for k in (i, i + 1):
                        if k < 16:
                            transpose_x(k, DUMMIES[d] if k % 2 == 0 else 0)
                    for k in z_runs.get(d, []):
                        transpose_z(k)
                    for k in z_runs.get(d, []):
                        collect_z(k)
                    for v in (i - 6, i - 5):
                        if 0 <= v < NQ:
                            product(v)
                    for k in score_runs.get(d, []):
                        score(k)
                        relu(k)
                if i < 16:
                    collect_x(i)
                if 0 <= i - 7 < NQ:
                    frames(i - 7)
                if 0 <= i - 8 < NQ:
                    squares(i - 8)
                if i % 2 == 1 and 3 <= i <= 17:
                    quantize_x((i - 3) // 2)
                if i == 2:
                    quantize(aw_codes[:], aw_sc[:], aw_grp[:].rearrange("p h j -> p (h j)"))
                if i in zq_steps:
                    quantize_z(zq_steps[i])
                if i in aq_steps:
                    quantize_a(aq_steps[i])
                for unit in range(7):
                    if i == 4 * unit + 11:
                        quantize_f(unit, whole)
                    if i == 4 * unit + 12 and EI_ENGINE[unit] != "g":
                        interleave(unit, whole, EI_ENGINE[unit])
                    if 4 * unit + 8 <= i < 4 * unit + 12 and EI_ENGINE[unit] == "g":
                        j = i - 4 * unit - 8
                        interleave(unit, slice(CH * j, CH * (j + 1)), "g")
                    if i == 4 * unit + 13:
                        quantize_e(unit, whole)
                if i == 37:
                    quantize_f(7, slice(0, 256))
                if i == 38:
                    interleave(7, slice(0, 128), "g")
                    interleave(7, slice(128, 256), "g")
                if i == 39:
                    quantize_f(7, slice(256, 512))
                    quantize_e(7, slice(0, 256))
                if i == 40:
                    pool_last((0, 1))
                    interleave(7, slice(256, 384), "g")
                    interleave(7, slice(384, 512), "v")
                    quantize_e(7, slice(256, 512))
                    pool_last((2, 3))
                    emit_last()
                if i == 18:
                    pool_half(0)
                if i == 19:
                    pool_half(1)
                if i == 22:
                    pool_half(2)
                if i == 26:
                    pool_half(3)
                if i == 27:
                    emit_half(0, 0)
                    emit_half(1, 0)
                if i == 28:
                    emit_half(0, 1)
                    emit_half(1, 1)
                if i in (30, 34, 38):
                    pool_chunk((i - 14) // 4)
                if i in (31, 35, 39):
                    emit_chunk((i - 15) // 4, False)
